import numpy as np
import ml_dtypes


def mxq(x, axis, fmt="e4m3"):
    dtype, down = {"e4m3": (ml_dtypes.float8_e4m3fn, 7), "e5m2": (ml_dtypes.float8_e5m2, 14)}[fmt]
    v = np.moveaxis(np.asarray(x, np.float32).astype(ml_dtypes.bfloat16).astype(np.float64), axis, -1)
    blocks = v.reshape(v.shape[:-1] + (-1, 32))
    amax = np.abs(blocks).max(-1, keepdims=True)
    byte = np.maximum(np.where(amax > 0, np.frexp(amax)[1] - 1 + 127, 0) - down, 1)
    scale = np.exp2(byte - 127.0)
    codes = (blocks / scale).astype(np.float32).astype(dtype).astype(np.float64)
    return np.moveaxis((codes * scale).reshape(v.shape), -1, axis)


WIDE = False


def mx_kscale(k):
    if not WIDE:
        return np.ones(k)
    levels = np.array([30, -30])
    if k % 512:
        return np.exp2(np.random.permutation(np.resize(levels, k // 32))).repeat(32)
    a = np.empty((k // 512, 16))
    for p in range(k // 512):
        a[p, :8] = np.random.permutation(np.resize(levels, 8))
        for g in range(8):
            far = levels[np.abs(levels - a[p, g]) >= 10]
            a[p, g + 8] = far[np.random.randint(len(far))]
    return np.exp2(a.ravel()).repeat(32)


def f64(x):
    return np.asarray(x).astype(np.float64)


def striped(idx):
    return np.tile(np.asarray(idx).reshape(-1, 16).T, (8, 1)).astype(np.uint16)


def unstriped(offs):
    return offs[:16].T.reshape(-1).astype(np.int64)


E2M1 = np.array([0.0, 0.5, 1.0, 1.5, 2.0, 3.0, 4.0, 6.0, -0.0, -0.5, -1.0, -1.5, -2.0, -3.0, -4.0, -6.0])


def pack_weight(w, fmt):
    k, n = w.shape
    w = f64(np.asarray(w, np.float32).astype(ml_dtypes.bfloat16)).reshape(k // 32, 32, n)
    amax = np.abs(w).max(1)
    if fmt in ("e4m3", "e5m2"):
        byte = np.frexp(amax)[1] - 1 + 127 - (7 if fmt == "e4m3" else 14)
    else:
        mant, ex = np.frexp(amax / 6.0)
        byte = np.where(mant > 0.5, ex, ex - 1) + 127
    byte = np.clip(np.where(amax > 0, byte, 1), 1, 254)
    scaled = (w * np.exp2(127.0 - byte)[:, None, :]).reshape(k, n).astype(np.float32)
    by_word = np.ascontiguousarray(scaled.reshape(k // 512, 128, 4, n).transpose(0, 1, 3, 2))
    if fmt in ("e4m3", "e5m2"):
        words = by_word.astype(ml_dtypes.float8_e4m3fn if fmt == "e4m3" else ml_dtypes.float8_e5m2).view(np.uint8)
    else:
        c = by_word.astype(ml_dtypes.float4_e2m1fn).view(np.uint8) & 0xF
        words = (c[..., 0::2] | (c[..., 1::2] << 4)).reshape(k // 512, 128, 2 * n)
    return np.ascontiguousarray(words), np.ascontiguousarray(byte.astype(np.uint8).reshape(k // 512, 16, n))


def unpack_weight(words, scales, fmt):
    g, _, n = scales.shape
    words = np.ascontiguousarray(words).reshape(g, 128, n, -1)
    if fmt in ("e4m3", "e5m2"):
        vals = words.view(ml_dtypes.float8_e4m3fn if fmt == "e4m3" else ml_dtypes.float8_e5m2).astype(np.float64)
    else:
        nib = np.empty((g, 128, n, 4), np.uint8)
        nib[..., 0::2] = words & 0xF
        nib[..., 1::2] = words >> 4
        vals = E2M1[nib]
    vals = vals * np.repeat(np.exp2(scales.astype(np.float64) - 127.0), 8, axis=1)[..., None]
    return vals.transpose(0, 1, 3, 2).reshape(g * 512, n)


K, T, J, I, R, C = 512, 512, 256, 256, 512, 512


def setup_inputs():
    n = np.random.standard_normal
    idx = np.random.permutation(T)[:J]
    idx2 = np.random.permutation(C)[:J]
    idx3 = np.random.permutation(T)[:I]
    fk = mx_kscale(K)
    fr = mx_kscale(R)
    xtp = pack_weight(n((K, T)) / fk[:, None], "e2m1")
    wap = pack_weight(n((K, R)) * 0.5 / np.sqrt(K) * fk[:, None] * fr, "e5m2")
    wbp = pack_weight(n((K, R)) * 1 / np.sqrt(K) * fk[:, None] / fr, "e4m3")
    return {
        "xt_words": xtp[0],
        "xt_scales": xtp[1],
        "wa_words": wap[0],
        "wa_scales": wap[1],
        "tf": (n((R, C))).astype(np.float32),
        "wb_words": wbp[0],
        "wb_scales": wbp[1],
        "offs": striped(idx),
        "offs2": striped(idx2),
        "offs3": striped(idx3),
    }


def reference(xt_words, xt_scales, wa_words, wa_scales, tf, wb_words, wb_scales, offs, offs2, offs3):
    idx = unstriped(offs)
    idx2 = unstriped(offs2)
    idx3 = unstriped(offs3)
    xtu = unpack_weight(xt_words, xt_scales, "e2m1")
    wau = unpack_weight(wa_words, wa_scales, "e5m2")
    wbu = unpack_weight(wb_words, wb_scales, "e4m3")
    xtidxg = xtu[:, idx]
    za = wau.T @ xtidxg
    ha = za * f64(tf)[:, idx2]
    xtidx3g = xtu[:, idx3]
    zb = wbu.T @ xtidx3g
    yb1 = np.pad(zb, ((0, 0), (1, 0)))[:, :I]
    hb = zb - 0.6 * yb1
    haq = mxq(ha, 0, "e5m2")
    hbq = mxq(hb, 0, "e5m2")
    a0 = haq.T @ hbq
    mn = np.mean(a0, axis=1, keepdims=True)
    y = 0.04 * np.maximum(a0 - mn, 0.0)
    return y

@@ -1,0 +1,178 @@
+from contextlib import ExitStack
+
+import concourse.mybir as mybir
+
+F32 = mybir.dt.float32
+BF16 = mybir.dt.bfloat16
+I32 = mybir.dt.int32
+U32 = mybir.dt.uint32
+U16 = mybir.dt.uint16
+U8 = mybir.dt.uint8
+E2M1 = mybir.dt.float4_e2m1fn_x4
+E4M3 = mybir.dt.float8_e4m3fn_x4
+E5M2 = mybir.dt.float8_e5m2_x4
+ALU = mybir.AluOpType
+ACT = mybir.ActivationFunctionType
+
+K, T, J, I, R, C = 512, 512, 256, 256, 512, 512
+P = 128
+SLOTS = 4
+HALF = 128
+LAG = 0.6
+GAIN = 0.04
+FLOPS = 2 * K * R * J + 2 * K * R * I + 2 * R * J * I
+
+
+def tile_list_meet_timestable_lagged_abovemean_kernel(
+    tc, xt_words, xt_scales, wa_words, wa_scales, tf, wb_words, wb_scales, offs, offs2, offs3, out
+):
+    nc = tc.nc
+    with ExitStack() as ctx:
+        sb = ctx.enter_context(tc.tile_pool(name="sb", bufs=1))
+        ps = ctx.enter_context(tc.psum_pool(name="ps", bufs=1))
+
+        def tile(shape, dtype, name):
+            return sb.tile(shape, dtype, name=name, align_bytes=64)
+
+        list_a = tile([P, J // 16], U16, "list_a")
+        list_f = tile([P, J // 16], U16, "list_f")
+        list_b = tile([P, I // 16], U16, "list_b")
+        x_words = tile([P, T], U16, "x_words")
+        x_scales = tile([P, T], U8, "x_scales")
+        wa_raw = tile([P, R], I32, "wa_raw")
+        wb_raw = tile([P, R], I32, "wb_raw")
+        wa_rows = tile([P, R // 4], I32, "wa_rows")
+        wb_rows = tile([P, R // 4], I32, "wb_rows")
+        wa_codes = tile([P, R], I32, "wa_codes")
+        wb_codes = tile([P, R], I32, "wb_codes")
+        wa_plane = tile([P, R], U8, "wa_plane")
+        wb_plane = tile([P, R], U8, "wb_plane")
+        tf_sb = [tile([P, C], F32, "tf_sb%d" % t) for t in range(SLOTS)]
+        lagged = tile([P, (I + 1) * SLOTS], F32, "lagged")
+
+        nc.vector.memset(x_scales[:].bitcast(I32), 0)
+        nc.vector.memset(wb_rows[:], 0)
+        nc.vector.memset(wa_rows[:], 0)
+        nc.vector.memset(lagged[:, 0:SLOTS], 0.0)
+
+        def load_scale_rows(dst, scales, queues):
+            rows = scales[0].bitcast(I32)
+            for q in range(4):
+                queues[q % len(queues)].dma_start(dst[32 * q : 32 * q + 4, :], rows[4 * q : 4 * q + 4, :])
+
+        tf_rows = tf.rearrange("(b t q) c -> t b q c", t=SLOTS, q=8)
+        nc.sync.dma_start(list_b[:], offs3)
+        nc.scalar.dma_start(x_words[:].bitcast(I32), xt_words[0].bitcast(I32))
+        load_scale_rows(x_scales[:].bitcast(I32), xt_scales, [nc.sync, nc.scalar])
+        nc.sync.dma_start(list_a[:], offs)
+        nc.scalar.dma_start(wb_raw[:], wb_words[0].rearrange("p n t -> p (n t)").bitcast(I32))
+        load_scale_rows(wb_rows[:], wb_scales, [nc.sync])
+        nc.sync.dma_start(list_f[:], offs2)
+        for t in range(2):
+            nc.sync.dma_start(tf_sb[t][:], tf_rows[t])
+        nc.sync.dma_start(wa_raw[:], wa_words[0].rearrange("p n t -> p (n t)").bitcast(I32))
+        load_scale_rows(wa_rows[:], wa_scales, [nc.sync])
+        for t in range(2, SLOTS):
+            nc.sync.dma_start(tf_sb[t][:], tf_rows[t])
+
+        def pick_tokens(offsets, name):
+            words = tile([P, J], U16, name + "_words")
+            scales = tile([P, J], U8, name + "_scales")
+            nc.vector.tensor_copy(words[:], x_words[:].indirect(offsets[:]))
+            nc.vector.tensor_copy(scales[:], x_scales[:].indirect(offsets[:]))
+            return words, scales
+
+        def deal_weight(raw, rows, codes, plane):
+            nc.vector.tensor_copy(
+                codes[:].rearrange("p (t b q) -> p t b q", t=SLOTS, q=8),
+                raw[:].rearrange("p (b t q) -> p t b q", t=SLOTS, q=8),
+            )
+            nc.vector.tensor_copy(
+                plane[:].bitcast(I32).rearrange("p (t b w) -> p t b w", t=SLOTS, w=2),
+                rows.rearrange("p (b t w) -> p t b w", t=SLOTS, w=2),
+            )
+
+        def project(codes, plane, fmt, words, scales, name):
+            banks = []
+            for h in range(2):
+                bank = ps.tile([P, SLOTS, HALF], F32, name="%s%d" % (name, h))
+                cols = slice(h * HALF, (h + 1) * HALF)
+                for t in range(SLOTS):
+                    rows = slice(t * P, (t + 1) * P)
+                    nc.tensor.matmul_mx(
+                        out=bank[:, t, :],
+                        lhsT=codes[:, rows].bitcast(fmt),
+                        lhsT_scale=plane[:, rows],
+                        rhs=words[:, cols].bitcast(E2M1),
+                        rhs_scale=scales[:, cols],
+                        start=True,
+                        stop=True,
+                    )
+                banks.append(bank)
+            return banks
+
+        xb_words, xb_scales = pick_tokens(list_b, "xb")
+        deal_weight(wb_raw, wb_rows[:], wb_codes, wb_plane)
+        zb = project(wb_codes, wb_plane, E4M3, xb_words, xb_scales, "zb")
+        for h in range(2):
+            lo = (h * HALF + 1) * SLOTS
+            nc.scalar.copy(
+                lagged[:, lo : lo + HALF * SLOTS].rearrange("p (i t) -> p i t", t=SLOTS),
+                zb[h][:].rearrange("p t i -> p i t"),
+            )
+
+        xa_words, xa_scales = pick_tokens(list_a, "xa")
+        deal_weight(wa_raw, wa_rows[:], wa_codes, wa_plane)
+        za = project(wa_codes, wa_plane, E5M2, xa_words, xa_scales, "za")
+
+        tf_picked = [tile([P, SLOTS, HALF], F32, "tf_picked%d" % h) for h in range(2)]
+        for h in range(2):
+            entries = list_f[:, h * HALF // 16 : (h + 1) * HALF // 16]
+            for t in range(SLOTS):
+                nc.scalar.activation(tf_picked[h][:, t, :], tf_sb[t][:].indirect(entries), ACT.Copy)
+
+        hb = tile([P, I * SLOTS], BF16, "hb")
+        for h in range(2):
+            lo, hi = h * HALF * SLOTS, (h + 1) * HALF * SLOTS
+            nc.vector.scalar_tensor_tensor(
+                hb[:, lo:hi], lagged[:, lo:hi], -LAG, lagged[:, lo + SLOTS : hi + SLOTS], ALU.mult, ALU.add
+            )
+        hb_codes = tile([P, I], U32, "hb_codes")
+        hb_plane = tile([P, I], U8, "hb_plane")
+        ha_codes = tile([P, J], U32, "ha_codes")
+        ha_plane = tile([P, J], U8, "ha_plane")
+        ha = [tile([P, HALF * SLOTS], BF16, "ha%d" % h) for h in range(2)]
+
+        def times_table(h):
+            nc.vector.tensor_tensor(
+                ha[h][:].rearrange("p (c e t) -> p c t e", e=2, t=SLOTS),
+                za[h][:].rearrange("p t (c e) -> p c t e", e=2),
+                tf_picked[h][:].rearrange("p t (c e) -> p c t e", e=2),
+                ALU.mult,
+            )
+
+        def finish(h):
+            cols = slice(h * HALF, (h + 1) * HALF)
+            nc.vector.quantize_mx(out=ha_codes[:, cols].bitcast(E5M2), scales=ha_plane[:, cols], in_=ha[h][:])
+            a0 = ps.tile([P, I], F32, name="a0_%d" % h)
+            nc.tensor.matmul_mx(
+                out=a0[:],
+                lhsT=ha_codes[:, cols].bitcast(E5M2),
+                lhsT_scale=ha_plane[:, cols],
+                rhs=hb_codes[:].bitcast(E5M2),
+                rhs_scale=hb_plane[:],
+                start=True,
+                stop=True,
+            )
+            share = tile([P, I], F32, "share%d" % h)
+            neg_mean = tile([P, 1], F32, "neg_mean%d" % h)
+            y = tile([P, I], F32, "y%d" % h)
+            nc.scalar.activation(share[:], a0[:], ACT.Copy, scale=-GAIN / I, accum_out=neg_mean[:])
+            nc.scalar.activation(y[:], share[:], ACT.Relu, bias=neg_mean[:], scale=-float(I))
+            nc.sync.dma_start(out[cols, :], y[:])
+
+        times_table(0)
+        nc.vector.quantize_mx(out=hb_codes[:].bitcast(E5M2), scales=hb_plane[:], in_=hb[:])
+        finish(0)
+        times_table(1)
+        finish(1)

@@ -31,8 +31,8 @@ def tile_list_meet_timestable_lagged_abovemean_kernel(
         sb = ctx.enter_context(tc.tile_pool(name="sb", bufs=1))
         ps = ctx.enter_context(tc.psum_pool(name="ps", bufs=1))
 
-        def tile(shape, dtype, name):
-            return sb.tile(shape, dtype, name=name, align_bytes=64)
+        def tile(shape, dtype, name, tag=None):
+            return sb.tile(shape, dtype, name=name, tag=tag or name, align_bytes=64)
 
         list_a = tile([P, J // 16], U16, "list_a")
         list_f = tile([P, J // 16], U16, "list_f")
@@ -49,47 +49,48 @@ def tile_list_meet_timestable_lagged_abovemean_kernel(
         wb_plane = tile([P, R], U8, "wb_plane")
         tf_sb = [tile([P, C], F32, "tf_sb%d" % t) for t in range(SLOTS)]
         lagged = tile([P, (I + 1) * SLOTS], F32, "lagged")
+        xb_words = tile([P, I], U16, "xb_words")
+        xb_scales = tile([P, I], U8, "xb_scales")
+        hb_codes = tile([P, I], U32, "hb_codes")
+        hb_plane = tile([P, I], U8, "hb_plane")
+        ha_codes = tile([P, J], U32, "ha_codes")
+        ha_plane = tile([P, J], U8, "ha_plane")
+        ha = [tile([P, HALF * SLOTS], BF16, "ha%d" % h) for h in range(2)]
+        tf_picked = tile([P, SLOTS, J], F32, "tf_picked")
 
         nc.vector.memset(x_scales[:].bitcast(I32), 0)
         nc.vector.memset(wb_rows[:], 0)
         nc.vector.memset(wa_rows[:], 0)
         nc.vector.memset(lagged[:, 0:SLOTS], 0.0)
 
-        def load_scale_rows(dst, scales, queues):
-            rows = scales[0].bitcast(I32)
-            for q in range(4):
-                queues[q % len(queues)].dma_start(dst[32 * q : 32 * q + 4, :], rows[4 * q : 4 * q + 4, :])
-
         tf_rows = tf.rearrange("(b t q) c -> t b q c", t=SLOTS, q=8)
         nc.sync.dma_start(list_b[:], offs3)
         nc.scalar.dma_start(x_words[:].bitcast(I32), xt_words[0].bitcast(I32))
-        load_scale_rows(x_scales[:].bitcast(I32), xt_scales, [nc.sync, nc.scalar])
-        nc.sync.dma_start(list_a[:], offs)
-        nc.scalar.dma_start(wb_raw[:], wb_words[0].rearrange("p n t -> p (n t)").bitcast(I32))
-        load_scale_rows(wb_rows[:], wb_scales, [nc.sync])
         nc.sync.dma_start(list_f[:], offs2)
-        for t in range(2):
-            nc.sync.dma_start(tf_sb[t][:], tf_rows[t])
+        nc.scalar.dma_start(x_scales[32:36, :].bitcast(I32), xt_scales[0].bitcast(I32)[4:8, :])
+        nc.sync.dma_start(x_scales[0:4, :].bitcast(I32), xt_scales[0].bitcast(I32)[0:4, :])
+        nc.scalar.dma_start(x_scales[96:100, :].bitcast(I32), xt_scales[0].bitcast(I32)[12:16, :])
+        nc.sync.dma_start(x_scales[64:68, :].bitcast(I32), xt_scales[0].bitcast(I32)[8:12, :])
+        nc.scalar.dma_start(wb_raw[:], wb_words[0].rearrange("p n t -> p (n t)").bitcast(I32))
+        nc.sync.dma_start(wb_rows[0:4, :], wb_scales[0].bitcast(I32)[0:4, :])
+        nc.scalar.dma_start(wb_rows[32:36, :], wb_scales[0].bitcast(I32)[4:8, :])
+        nc.sync.dma_start(wb_rows[64:68, :], wb_scales[0].bitcast(I32)[8:12, :])
+        nc.scalar.dma_start(wb_rows[96:100, :], wb_scales[0].bitcast(I32)[12:16, :])
+        nc.sync.dma_start(list_a[:], offs)
+        nc.scalar.dma_start(tf_sb[0][:], tf_rows[0])
         nc.sync.dma_start(wa_raw[:], wa_words[0].rearrange("p n t -> p (n t)").bitcast(I32))
-        load_scale_rows(wa_rows[:], wa_scales, [nc.sync])
-        for t in range(2, SLOTS):
-            nc.sync.dma_start(tf_sb[t][:], tf_rows[t])
+        nc.scalar.dma_start(tf_sb[1][:], tf_rows[1])
+        nc.sync.dma_start(wa_rows[0:4, :], wa_scales[0].bitcast(I32)[0:4, :])
+        nc.sync.dma_start(wa_rows[32:36, :], wa_scales[0].bitcast(I32)[4:8, :])
+        nc.sync.dma_start(wa_rows[64:68, :], wa_scales[0].bitcast(I32)[8:12, :])
+        nc.sync.dma_start(wa_rows[96:100, :], wa_scales[0].bitcast(I32)[12:16, :])
+        nc.sync.dma_start(tf_sb[2][:], tf_rows[2])
+        nc.sync.dma_start(tf_sb[3][:], tf_rows[3])
 
-        def pick_tokens(offsets, name):
-            words = tile([P, J], U16, name + "_words")
-            scales = tile([P, J], U8, name + "_scales")
-            nc.vector.tensor_copy(words[:], x_words[:].indirect(offsets[:]))
-            nc.vector.tensor_copy(scales[:], x_scales[:].indirect(offsets[:]))
-            return words, scales
-
-        def deal_weight(raw, rows, codes, plane):
-            nc.vector.tensor_copy(
-                codes[:].rearrange("p (t b q) -> p t b q", t=SLOTS, q=8),
-                raw[:].rearrange("p (b t q) -> p t b q", t=SLOTS, q=8),
-            )
-            nc.vector.tensor_copy(
-                plane[:].bitcast(I32).rearrange("p (t b w) -> p t b w", t=SLOTS, w=2),
-                rows.rearrange("p (b t w) -> p t b w", t=SLOTS, w=2),
+        def deal(engine, dst, src, run):
+            engine.tensor_copy(
+                dst.rearrange("p (t b q) -> p t b q", t=SLOTS, q=run),
+                src.rearrange("p (b t q) -> p t b q", t=SLOTS, q=run),
             )
 
         def project(codes, plane, fmt, words, scales, name):
@@ -111,49 +112,33 @@ def tile_list_meet_timestable_lagged_abovemean_kernel(
                 banks.append(bank)
             return banks
 
-        xb_words, xb_scales = pick_tokens(list_b, "xb")
-        deal_weight(wb_raw, wb_rows[:], wb_codes, wb_plane)
-        zb = project(wb_codes, wb_plane, E4M3, xb_words, xb_scales, "zb")
-        for h in range(2):
+        def unload(h):
             lo = (h * HALF + 1) * SLOTS
             nc.scalar.copy(
                 lagged[:, lo : lo + HALF * SLOTS].rearrange("p (i t) -> p i t", t=SLOTS),
                 zb[h][:].rearrange("p t i -> p i t"),
             )
 
-        xa_words, xa_scales = pick_tokens(list_a, "xa")
-        deal_weight(wa_raw, wa_rows[:], wa_codes, wa_plane)
-        za = project(wa_codes, wa_plane, E5M2, xa_words, xa_scales, "za")
-
-        tf_picked = [tile([P, SLOTS, HALF], F32, "tf_picked%d" % h) for h in range(2)]
-        for h in range(2):
-            entries = list_f[:, h * HALF // 16 : (h + 1) * HALF // 16]
-            for t in range(SLOTS):
-                nc.scalar.activation(tf_picked[h][:, t, :], tf_sb[t][:].indirect(entries), ACT.Copy)
-
-        hb = tile([P, I * SLOTS], BF16, "hb")
-        for h in range(2):
+        def lag(h):
             lo, hi = h * HALF * SLOTS, (h + 1) * HALF * SLOTS
             nc.vector.scalar_tensor_tensor(
                 hb[:, lo:hi], lagged[:, lo:hi], -LAG, lagged[:, lo + SLOTS : hi + SLOTS], ALU.mult, ALU.add
             )
-        hb_codes = tile([P, I], U32, "hb_codes")
-        hb_plane = tile([P, I], U8, "hb_plane")
-        ha_codes = tile([P, J], U32, "ha_codes")
-        ha_plane = tile([P, J], U8, "ha_plane")
-        ha = [tile([P, HALF * SLOTS], BF16, "ha%d" % h) for h in range(2)]
 
         def times_table(h):
             nc.vector.tensor_tensor(
                 ha[h][:].rearrange("p (c e t) -> p c t e", e=2, t=SLOTS),
                 za[h][:].rearrange("p t (c e) -> p c t e", e=2),
-                tf_picked[h][:].rearrange("p t (c e) -> p c t e", e=2),
+                tf_picked[:, :, h * HALF : (h + 1) * HALF].rearrange("p t (c e) -> p c t e", e=2),
                 ALU.mult,
             )
 
-        def finish(h):
+        def quantise_rows(h):
             cols = slice(h * HALF, (h + 1) * HALF)
             nc.vector.quantize_mx(out=ha_codes[:, cols].bitcast(E5M2), scales=ha_plane[:, cols], in_=ha[h][:])
+
+        def finish(h):
+            cols = slice(h * HALF, (h + 1) * HALF)
             a0 = ps.tile([P, I], F32, name="a0_%d" % h)
             nc.tensor.matmul_mx(
                 out=a0[:],
@@ -167,12 +152,42 @@ def tile_list_meet_timestable_lagged_abovemean_kernel(
             share = tile([P, I], F32, "share%d" % h)
             neg_mean = tile([P, 1], F32, "neg_mean%d" % h)
             y = tile([P, I], F32, "y%d" % h)
-            nc.scalar.activation(share[:], a0[:], ACT.Copy, scale=-GAIN / I, accum_out=neg_mean[:])
+            if h == 0:
+                nc.scalar.activation(share[:], a0[:], ACT.Copy, scale=-GAIN / I, accum_out=neg_mean[:])
+            else:
+                nc.vector.tensor_scalar(share[:], a0[:], -GAIN / I, None, ALU.mult, ALU.add, accum_out=neg_mean[:])
             nc.scalar.activation(y[:], share[:], ACT.Relu, bias=neg_mean[:], scale=-float(I))
             nc.sync.dma_start(out[cols, :], y[:])
 
+        nc.vector.tensor_copy(xb_words[:], x_words[:].indirect(list_b[:]))
+        nc.vector.tensor_copy(xb_scales[:], x_scales[:].indirect(list_b[:]))
+        deal(nc.vector, wb_codes[:], wb_raw[:], 8)
+        deal(nc.vector, wb_plane[:].bitcast(I32), wb_rows[:], 2)
+        zb = project(wb_codes, wb_plane, E4M3, xb_words, xb_scales, "zb")
+        nc.scalar.activation(tf_picked[:, 0, :], tf_sb[0][:].indirect(list_f[:]), ACT.Copy)
+        unload(0)
+        unload(1)
+        xa_words = tile([P, J], U16, "xa_words")
+        nc.vector.tensor_copy(xa_words[:], x_words[:].indirect(list_a[:]))
+        xa_scales = tile([P, J], U8, "xa_scales")
+        nc.vector.tensor_copy(xa_scales[:], x_scales[:].indirect(list_a[:]))
+        deal(nc.vector, wa_codes[:], wa_raw[:], 8)
+        nc.vector.tensor_copy(tf_picked[:, 1, 128:256], tf_sb[1][:].indirect(list_f[:, 8:16]))
+        deal(nc.vector, wa_plane[:].bitcast(I32), wa_rows[:], 2)
+        za = project(wa_codes, wa_plane, E5M2, xa_words, xa_scales, "za")
+        nc.scalar.activation(tf_picked[:, 1, 0:128], tf_sb[1][:].indirect(list_f[:, 0:8]), ACT.Copy)
+        nc.scalar.activation(tf_picked[:, 2, :], tf_sb[2][:].indirect(list_f[:]), ACT.Copy)
+        nc.scalar.activation(tf_picked[:, 3, 0:128], tf_sb[3][:].indirect(list_f[:, 0:8]), ACT.Copy)
+        nc.scalar.activation(tf_picked[:, 3, 128:256], tf_sb[3][:].indirect(list_f[:, 8:16]), ACT.Copy)
+        hb = tile([P, I * SLOTS], BF16, "hb", tag="wa_rows")
+        lag(0)
+        lag(1)
+        for h in range(2):
+            cols = slice(h * HALF, (h + 1) * HALF)
+            nc.vector.quantize_mx(out=hb_codes[:, cols].bitcast(E5M2), scales=hb_plane[:, cols], in_=hb[:, h * HALF * SLOTS : (h + 1) * HALF * SLOTS])
         times_table(0)
-        nc.vector.quantize_mx(out=hb_codes[:].bitcast(E5M2), scales=hb_plane[:], in_=hb[:])
-        finish(0)
         times_table(1)
+        quantise_rows(0)
+        quantise_rows(1)
+        finish(0)
         finish(1)

from contextlib import ExitStack

import concourse.mybir as mybir

F32 = mybir.dt.float32
BF16 = mybir.dt.bfloat16
I32 = mybir.dt.int32
U32 = mybir.dt.uint32
U16 = mybir.dt.uint16
U8 = mybir.dt.uint8
E2M1 = mybir.dt.float4_e2m1fn_x4
E4M3 = mybir.dt.float8_e4m3fn_x4
E5M2 = mybir.dt.float8_e5m2_x4
ALU = mybir.AluOpType
ACT = mybir.ActivationFunctionType

K, T, J, I, R, C = 512, 512, 256, 256, 512, 512
P = 128
SLOTS = 4
HALF = 128
LAG = 0.6
GAIN = 0.04
FLOPS = 2 * K * R * J + 2 * K * R * I + 2 * R * J * I


def tile_list_meet_timestable_lagged_abovemean_kernel(
    tc, xt_words, xt_scales, wa_words, wa_scales, tf, wb_words, wb_scales, offs, offs2, offs3, out
):
    nc = tc.nc
    with ExitStack() as ctx:
        sb = ctx.enter_context(tc.tile_pool(name="sb", bufs=1))
        ps = ctx.enter_context(tc.psum_pool(name="ps", bufs=1))

        def tile(shape, dtype, name, tag=None):
            return sb.tile(shape, dtype, name=name, tag=tag or name, align_bytes=64)

        list_a = tile([P, J // 16], U16, "list_a")
        list_f = tile([P, J // 16], U16, "list_f")
        list_b = tile([P, I // 16], U16, "list_b")
        x_words = tile([P, T], U16, "x_words")
        x_scales = tile([P, T], U8, "x_scales")
        wa_raw = tile([P, R], I32, "wa_raw")
        wb_raw = tile([P, R], I32, "wb_raw")
        wa_rows = tile([P, R // 4], I32, "wa_rows")
        wb_rows = tile([P, R // 4], I32, "wb_rows")
        wa_codes = tile([P, R], I32, "wa_codes")
        wb_codes = tile([P, R], I32, "wb_codes")
        wa_plane = tile([P, R], U8, "wa_plane")
        wb_plane = tile([P, R], U8, "wb_plane")
        tf_sb = [tile([P, C], F32, "tf_sb%d" % t) for t in range(SLOTS)]
        lagged = tile([P, (I + 1) * SLOTS], F32, "lagged")
        xb_words = tile([P, I], U16, "xb_words")
        xb_scales = tile([P, I], U8, "xb_scales")
        hb_codes = tile([P, I], U32, "hb_codes")
        hb_plane = tile([P, I], U8, "hb_plane")
        ha_codes = tile([P, J], U32, "ha_codes")
        ha_plane = tile([P, J], U8, "ha_plane")
        ha = [tile([P, HALF * SLOTS], BF16, "ha%d" % h) for h in range(2)]
        tf_picked = tile([P, SLOTS, J], F32, "tf_picked")

        nc.vector.memset(x_scales[:].bitcast(I32), 0)
        nc.vector.memset(wb_rows[:], 0)
        nc.vector.memset(wa_rows[:], 0)
        nc.vector.memset(lagged[:, 0:SLOTS], 0.0)

        tf_rows = tf.rearrange("(b t q) c -> t b q c", t=SLOTS, q=8)
        nc.sync.dma_start(list_b[:], offs3)
        nc.scalar.dma_start(x_words[:].bitcast(I32), xt_words[0].bitcast(I32))
        nc.sync.dma_start(list_f[:], offs2)
        nc.scalar.dma_start(x_scales[32:36, :].bitcast(I32), xt_scales[0].bitcast(I32)[4:8, :])
        nc.sync.dma_start(x_scales[0:4, :].bitcast(I32), xt_scales[0].bitcast(I32)[0:4, :])
        nc.scalar.dma_start(x_scales[96:100, :].bitcast(I32), xt_scales[0].bitcast(I32)[12:16, :])
        nc.sync.dma_start(x_scales[64:68, :].bitcast(I32), xt_scales[0].bitcast(I32)[8:12, :])
        nc.scalar.dma_start(wb_raw[:], wb_words[0].rearrange("p n t -> p (n t)").bitcast(I32))
        nc.sync.dma_start(wb_rows[0:4, :], wb_scales[0].bitcast(I32)[0:4, :])
        nc.scalar.dma_start(wb_rows[32:36, :], wb_scales[0].bitcast(I32)[4:8, :])
        nc.sync.dma_start(wb_rows[64:68, :], wb_scales[0].bitcast(I32)[8:12, :])
        nc.scalar.dma_start(wb_rows[96:100, :], wb_scales[0].bitcast(I32)[12:16, :])
        nc.sync.dma_start(list_a[:], offs)
        nc.scalar.dma_start(tf_sb[0][:], tf_rows[0])
        nc.sync.dma_start(wa_raw[:], wa_words[0].rearrange("p n t -> p (n t)").bitcast(I32))
        nc.scalar.dma_start(tf_sb[1][:], tf_rows[1])
        nc.sync.dma_start(wa_rows[0:4, :], wa_scales[0].bitcast(I32)[0:4, :])
        nc.sync.dma_start(wa_rows[32:36, :], wa_scales[0].bitcast(I32)[4:8, :])
        nc.sync.dma_start(wa_rows[64:68, :], wa_scales[0].bitcast(I32)[8:12, :])
        nc.sync.dma_start(wa_rows[96:100, :], wa_scales[0].bitcast(I32)[12:16, :])
        nc.sync.dma_start(tf_sb[2][:], tf_rows[2])
        nc.sync.dma_start(tf_sb[3][:], tf_rows[3])

        def deal(engine, dst, src, run):
            engine.tensor_copy(
                dst.rearrange("p (t b q) -> p t b q", t=SLOTS, q=run),
                src.rearrange("p (b t q) -> p t b q", t=SLOTS, q=run),
            )

        def project(codes, plane, fmt, words, scales, name):
            banks = []
            for h in range(2):
                bank = ps.tile([P, SLOTS, HALF], F32, name="%s%d" % (name, h))
                cols = slice(h * HALF, (h + 1) * HALF)
                for t in range(SLOTS):
                    rows = slice(t * P, (t + 1) * P)
                    nc.tensor.matmul_mx(
                        out=bank[:, t, :],
                        lhsT=codes[:, rows].bitcast(fmt),
                        lhsT_scale=plane[:, rows],
                        rhs=words[:, cols].bitcast(E2M1),
                        rhs_scale=scales[:, cols],
                        start=True,
                        stop=True,
                    )
                banks.append(bank)
            return banks

        def unload(h):
            lo = (h * HALF + 1) * SLOTS
            nc.scalar.copy(
                lagged[:, lo : lo + HALF * SLOTS].rearrange("p (i t) -> p i t", t=SLOTS),
                zb[h][:].rearrange("p t i -> p i t"),
            )

        def lag(h):
            lo, hi = h * HALF * SLOTS, (h + 1) * HALF * SLOTS
            nc.vector.scalar_tensor_tensor(
                hb[:, lo:hi], lagged[:, lo:hi], -LAG, lagged[:, lo + SLOTS : hi + SLOTS], ALU.mult, ALU.add
            )

        def times_table(h):
            nc.vector.tensor_tensor(
                ha[h][:].rearrange("p (c e t) -> p c t e", e=2, t=SLOTS),
                za[h][:].rearrange("p t (c e) -> p c t e", e=2),
                tf_picked[:, :, h * HALF : (h + 1) * HALF].rearrange("p t (c e) -> p c t e", e=2),
                ALU.mult,
            )

        def quantise_rows(h):
            cols = slice(h * HALF, (h + 1) * HALF)
            nc.vector.quantize_mx(out=ha_codes[:, cols].bitcast(E5M2), scales=ha_plane[:, cols], in_=ha[h][:])

        def finish(h):
            cols = slice(h * HALF, (h + 1) * HALF)
            a0 = ps.tile([P, I], F32, name="a0_%d" % h)
            nc.tensor.matmul_mx(
                out=a0[:],
                lhsT=ha_codes[:, cols].bitcast(E5M2),
                lhsT_scale=ha_plane[:, cols],
                rhs=hb_codes[:].bitcast(E5M2),
                rhs_scale=hb_plane[:],
                start=True,
                stop=True,
            )
            share = tile([P, I], F32, "share%d" % h)
            neg_mean = tile([P, 1], F32, "neg_mean%d" % h)
            y = tile([P, I], F32, "y%d" % h)
            if h == 0:
                nc.scalar.activation(share[:], a0[:], ACT.Copy, scale=-GAIN / I, accum_out=neg_mean[:])
            else:
                nc.vector.tensor_scalar(share[:], a0[:], -GAIN / I, None, ALU.mult, ALU.add, accum_out=neg_mean[:])
            nc.scalar.activation(y[:], share[:], ACT.Relu, bias=neg_mean[:], scale=-float(I))
            nc.sync.dma_start(out[cols, :], y[:])

        nc.vector.tensor_copy(xb_words[:], x_words[:].indirect(list_b[:]))
        nc.vector.tensor_copy(xb_scales[:], x_scales[:].indirect(list_b[:]))
        deal(nc.vector, wb_codes[:], wb_raw[:], 8)
        deal(nc.vector, wb_plane[:].bitcast(I32), wb_rows[:], 2)
        zb = project(wb_codes, wb_plane, E4M3, xb_words, xb_scales, "zb")
        nc.scalar.activation(tf_picked[:, 0, :], tf_sb[0][:].indirect(list_f[:]), ACT.Copy)
        unload(0)
        unload(1)
        xa_words = tile([P, J], U16, "xa_words")
        nc.vector.tensor_copy(xa_words[:], x_words[:].indirect(list_a[:]))
        xa_scales = tile([P, J], U8, "xa_scales")
        nc.vector.tensor_copy(xa_scales[:], x_scales[:].indirect(list_a[:]))
        deal(nc.vector, wa_codes[:], wa_raw[:], 8)
        nc.vector.tensor_copy(tf_picked[:, 1, 128:256], tf_sb[1][:].indirect(list_f[:, 8:16]))
        deal(nc.vector, wa_plane[:].bitcast(I32), wa_rows[:], 2)
        za = project(wa_codes, wa_plane, E5M2, xa_words, xa_scales, "za")
        nc.scalar.activation(tf_picked[:, 1, 0:128], tf_sb[1][:].indirect(list_f[:, 0:8]), ACT.Copy)
        nc.scalar.activation(tf_picked[:, 2, :], tf_sb[2][:].indirect(list_f[:]), ACT.Copy)
        nc.scalar.activation(tf_picked[:, 3, 0:128], tf_sb[3][:].indirect(list_f[:, 0:8]), ACT.Copy)
        nc.scalar.activation(tf_picked[:, 3, 128:256], tf_sb[3][:].indirect(list_f[:, 8:16]), ACT.Copy)
        hb = tile([P, I * SLOTS], BF16, "hb", tag="wa_rows")
        lag(0)
        lag(1)
        for h in range(2):
            cols = slice(h * HALF, (h + 1) * HALF)
            nc.vector.quantize_mx(out=hb_codes[:, cols].bitcast(E5M2), scales=hb_plane[:, cols], in_=hb[:, h * HALF * SLOTS : (h + 1) * HALF * SLOTS])
        times_table(0)
        times_table(1)
        quantise_rows(0)
        quantise_rows(1)
        finish(0)
        finish(1)
